import numpy as np
import ml_dtypes


def mxq(x, axis, fmt="e4m3"):
    dtype, down = {"e4m3": (ml_dtypes.float8_e4m3fn, 7), "e5m2": (ml_dtypes.float8_e5m2, 14)}[fmt]
    v = np.moveaxis(np.asarray(x, np.float32).astype(ml_dtypes.bfloat16).astype(np.float64), axis, -1)
    blocks = v.reshape(v.shape[:-1] + (-1, 32))
    amax = np.abs(blocks).max(-1, keepdims=True)
    byte = np.maximum(np.where(amax > 0, np.frexp(amax)[1] - 1 + 127, 0) - down, 1)
    scale = np.exp2(byte - 127.0)
    codes = (blocks / scale).astype(np.float32).astype(dtype).astype(np.float64)
    return np.moveaxis((codes * scale).reshape(v.shape), -1, axis)


WIDE = False


def mx_kscale(k):
    if not WIDE:
        return np.ones(k)
    levels = np.array([10, -10, 5, -5, 0])
    if k % 512:
        return np.exp2(np.random.permutation(np.resize(levels, k // 32))).repeat(32)
    a = np.empty((k // 512, 16))
    for p in range(k // 512):
        a[p, :8] = np.random.permutation(np.resize(levels, 8))
        for g in range(8):
            far = levels[np.abs(levels - a[p, g]) >= 10]
            a[p, g + 8] = far[np.random.randint(len(far))]
    return np.exp2(a.ravel()).repeat(32)


def f64(x):
    return np.asarray(x).astype(np.float64)


def striped(idx):
    return np.tile(idx.reshape(-1, 16).T, (8, 1)).astype(np.uint16)


def unstriped(offs):
    return offs[:16].T.reshape(-1).astype(np.int64)


def striped8(idx):
    return np.concatenate([x.reshape(-1, 16).T for x in idx]).astype(np.uint16)


def runs(offs, k):
    lists = np.stack([offs[16 * r : 16 * r + 16].T.reshape(-1) for r in range(8)]).astype(np.int64)
    return lists[np.arange(k) % 512 // 64]


def pack_weight(w):
    k, n = w.shape
    w = f64(np.asarray(w, np.float32).astype(ml_dtypes.bfloat16)).reshape(k // 32, 32, n)
    amax = np.abs(w).max(1)
    byte = np.clip(np.where(amax > 0, np.frexp(amax)[1] - 1 + 127 - 7, 1), 1, 254)
    scaled = (w * np.exp2(127.0 - byte)[:, None, :]).reshape(k, n).astype(np.float32)
    words = np.ascontiguousarray(scaled.reshape(k // 512, 128, 4, n).transpose(0, 1, 3, 2)).astype(ml_dtypes.float8_e4m3fn).view(np.uint8)
    return words, np.ascontiguousarray(byte.astype(np.uint8).reshape(k // 512, 16, n))


def unpack_weight(words, scales):
    g, p, n, _ = words.shape
    vals = np.ascontiguousarray(words).view(ml_dtypes.float8_e4m3fn).astype(np.float64) * np.repeat(np.exp2(scales.astype(np.float64) - 127.0), 8, axis=1)[..., None]
    return vals.transpose(0, 1, 3, 2).reshape(g * 512, n)


def sigmoid(v):
    return 1.0 / (1.0 + np.exp(-np.maximum(v, -700.0)))


K, T, S, N, H = 512, 2048, 512, 512, 512


def setup_inputs():
    n = np.random.standard_normal
    s = mx_kscale(K)[:, None]
    u = mx_kscale(S)
    packed_xT = pack_weight(n((K, T)) * s)
    return {
        "x_words": packed_xT[0],
        "x_scales": packed_xT[1],
        "wa": (n((K, H)) / np.sqrt(K) / s).astype(np.float32),
        "gt": (np.random.uniform(0.5, 1.5, (S, 1)) * u[:, None]).astype(np.float32),
        "w1": (n((S, N)) / np.sqrt(S) / u[:, None]).astype(np.float32),
        "offs": striped(np.random.permutation(T)[:S]),
        "n1": striped8(np.stack([np.random.permutation(H) for _ in range(8)])),
        "n2": striped8(np.stack([np.random.permutation(H) for _ in range(8)])),
        "n3": striped8(np.stack([np.random.permutation(H) for _ in range(8)])),
        "n4": striped8(np.stack([np.random.permutation(H) for _ in range(8)])),
    }


def reference(x_words, x_scales, wa, gt, w1, offs, n1, n2, n3, n4):
    xq = unpack_weight(x_words, x_scales)[:, unstriped(offs)]
    y = xq.T @ mxq(f64(wa), 0, "e4m3")
    z = f64(gt) * (y + (sigmoid(y[np.arange(S)[:, None], runs(n1, S)])) * (y[np.arange(S)[:, None], runs(n2, S)] - y))
    h = mxq(f64(w1), 0, "e4m3").T @ mxq(z, 0, "e4m3")
    return h * (h[np.arange(N)[:, None], runs(n3, N)] - (h[np.arange(N)[:, None], runs(n4, N)]))

@@ -1,0 +1,216 @@
+from contextlib import ExitStack
+
+import concourse.mybir as mybir
+
+K, T, S, N, H = 512, 2048, 512, 512, 512
+FLOPS = 2 * K * S * H + 2 * S * N * H
+
+F32 = mybir.dt.float32
+BF16 = mybir.dt.bfloat16
+I32 = mybir.dt.int32
+U32 = mybir.dt.uint32
+U16 = mybir.dt.uint16
+U8 = mybir.dt.uint8
+FP8X4 = mybir.dt.float8_e4m3fn_x4
+ALU = mybir.AluOpType
+ACT = mybir.ActivationFunctionType
+
+P = 128
+PACK = 4
+HALF = H // 2
+LIST_COLS = HALF // 16
+SCALAR_COLS = 96
+Z_CHUNKS = ((0, 256), (256, 384), (384, 512))
+H_EARLY = 384
+SCALE_ROW0 = P - 16
+
+
+def side_by_side(grouped, rows):
+    return (
+        grouped.rearrange("p (c i) j -> p c j i", i=4),
+        rows.rearrange("p j (c i) -> p c j i", i=4),
+    )
+
+
+def tile_picked_toktrackwind_none_p_kernel(
+    tc, x_words, x_scales, wa, gt, w1, offs, n1, n2, n3, n4, out
+):
+    nc = tc.nc
+    halves = [slice(h * HALF, (h + 1) * HALF) for h in range(2)]
+    list_halves = [slice(h * LIST_COLS, (h + 1) * LIST_COLS) for h in range(2)]
+
+    with ExitStack() as ctx:
+        keep = ctx.enter_context(tc.tile_pool(name="keep", bufs=1))
+        ring = ctx.enter_context(tc.tile_pool(name="ring", bufs=2))
+        psum = ctx.enter_context(tc.psum_pool(name="psum", bufs=1))
+
+        def load_list(source, name):
+            tile = keep.tile([P, source.shape[1]], U16, name=name)
+            nc.sync.dma_start(tile[:], source)
+            return tile
+
+        scale_table = keep.tile([P, T], U8, align_bytes=64)
+        nc.sync.dma_start(scale_table[SCALE_ROW0:, :].bitcast(I32), x_scales[0].bitcast(I32))
+        nc.vector.memset(scale_table[:SCALE_ROW0, :].bitcast(I32), 0)
+        x_scale = keep.tile([P, S], U8, align_bytes=64)
+        nc.vector.memset(x_scale[:].bitcast(I32), 0)
+        offs_t = load_list(offs, "offs_t")
+        word_table = keep.tile([P, T], I32, align_bytes=64)
+        nc.sync.dma_start(word_table[:], x_words[0].rearrange("p n r -> p (n r)").bitcast(I32))
+        wa_rows = wa.rearrange("(p j) c -> p j c", j=PACK)
+        wa_raw = []
+        for h in range(2):
+            raw = keep.tile([P, PACK, HALF], F32, name="wa_raw%d" % h)
+            nc.sync.dma_start(raw[:], wa_rows[:, :, halves[h]])
+            wa_raw.append(raw)
+        gain = keep.tile([P, PACK], F32)
+        nc.sync.dma_start(gain[:], gt.rearrange("(p t) o -> p (t o)", t=PACK))
+        n1_t = load_list(n1, "n1_t")
+        n2_t = load_list(n2, "n2_t")
+        w1_raw = keep.tile([P, PACK, N], F32)
+        nc.sync.dma_start(w1_raw[:], w1.rearrange("(p j) m -> p j m", j=PACK))
+        n3_t = load_list(n3, "n3_t")
+        n4_t = load_list(n4, "n4_t")
+
+        picked_scales = keep.tile([P, S], U8, align_bytes=64)
+        nc.vector.tensor_copy(picked_scales[:], scale_table[:].indirect(offs_t[:]))
+        dealt_scales = keep.tile([P, S], U8, align_bytes=64)
+        nc.vector.tensor_copy(
+            dealt_scales[:].rearrange("p (t m) -> p t m", t=PACK),
+            picked_scales[:].rearrange("p (m t) -> p t m", t=PACK),
+        )
+        for q in range(4):
+            nc.scalar.dma_start(
+                x_scale[32 * q : 32 * q + 4, :].bitcast(I32),
+                dealt_scales[SCALE_ROW0 + 4 * q : SCALE_ROW0 + 4 * q + 4, :].bitcast(I32),
+            )
+        x_codes = keep.tile([P, S], U32, align_bytes=64)
+        nc.vector.tensor_copy(
+            x_codes[:].rearrange("p (t m) -> p m t", t=PACK),
+            word_table[:].bitcast(U32).indirect(offs_t[:]),
+        )
+
+        y = [keep.tile([P, H], F32, name="y%d" % t, tag="y%d" % t, align_bytes=64) for t in range(PACK)]
+        gy = [keep.tile([P, H], F32, name="gy%d" % t) for t in range(PACK)]
+        y_banks = {}
+        for h in range(2):
+            grouped = keep.tile([P, HALF, PACK], BF16, name="wa_grouped%d" % h, align_bytes=64)
+            nc.scalar.copy(*side_by_side(grouped[:, :SCALAR_COLS, :], wa_raw[h][:, :, :SCALAR_COLS]))
+            nc.vector.tensor_copy(*side_by_side(grouped[:, SCALAR_COLS:, :], wa_raw[h][:, :, SCALAR_COLS:]))
+            codes = keep.tile([P, HALF], U32, name="wa_codes%d" % h, align_bytes=64)
+            scale = keep.tile([P, HALF], U8, name="wa_scale%d" % h, align_bytes=64)
+            nc.vector.quantize_mx(
+                out=codes[:].bitcast(FP8X4), scales=scale[:], in_=grouped[:].rearrange("p c j -> p (c j)")
+            )
+            for t in range(PACK):
+                bank = psum.tile([P, HALF], F32, name="y_bank", tag="bank%d_%d" % (h, t))
+                nc.tensor.matmul_mx(
+                    out=bank[:],
+                    lhsT=x_codes[:, t * P : (t + 1) * P].bitcast(FP8X4),
+                    lhsT_scale=x_scale[:, t * P : (t + 1) * P],
+                    rhs=codes[:].bitcast(FP8X4),
+                    rhs_scale=scale[:],
+                    start=True,
+                    stop=True,
+                )
+                y_banks[h, t] = bank
+
+        def gain_on_vector(t, h):
+            nc.vector.tensor_scalar(gy[t][:, halves[h]], y[t][:, halves[h]], gain[:, t : t + 1], None, ALU.mult)
+
+        for t in range(PACK):
+            nc.scalar.copy(y[t][:, halves[0]], y_banks[0, t][:])
+            gain_on_vector(t, 0)
+
+        taken = [keep.tile([P, PACK, HALF], F32, name="taken%d" % h) for h in range(2)]
+        kept = [keep.tile([P, PACK, HALF], F32, name="kept%d" % h) for h in range(2)]
+        for t in range(PACK):
+            nc.scalar.copy(y[t][:, halves[1]], y_banks[1, t][:])
+            if t == 0:
+                gain_on_vector(t, 1)
+            else:
+                nc.scalar.activation(gy[t][:, halves[1]], y_banks[1, t][:], ACT.Copy, scale=gain[:, t : t + 1])
+            for h in range(2):
+                gate = keep.tile([P, HALF], F32, name="gate%d_%d" % (t, h))
+                nc.scalar.activation(gate[:], y[t][:].indirect(n1_t[:, list_halves[h]]), ACT.Sigmoid)
+                nc.vector.tensor_tensor(
+                    taken[h][:, t, :], gy[t][:].indirect(n2_t[:, list_halves[h]]), gate[:], ALU.mult
+                )
+                nc.vector.scalar_tensor_tensor(
+                    kept[h][:, t, :], gate[:], 1.0, gy[t][:, halves[h]], ALU.subtract, ALU.mult
+                )
+
+        w1_grouped = keep.tile([P, N * PACK], BF16, tag="y2", align_bytes=64)
+        w1_dealt = w1_grouped[:].rearrange("p (t m j) -> p m j t", t=PACK, j=PACK)
+        w1_rows = w1_raw[:].rearrange("p j (m t) -> p m j t", t=PACK)
+        for h in range(2):
+            nc.scalar.copy(w1_dealt[:, h * 64 : (h + 1) * 64], w1_rows[:, h * 64 : (h + 1) * 64])
+        w1_codes = [keep.tile([P, P], U32, name="w1_codes%d" % t, align_bytes=64) for t in range(PACK)]
+        w1_scale = [keep.tile([P, P], U8, name="w1_scale%d" % t, align_bytes=64) for t in range(PACK)]
+
+        def quantise_w1(t):
+            nc.vector.quantize_mx(
+                out=w1_codes[t][:].bitcast(FP8X4), scales=w1_scale[t][:], in_=w1_grouped[:, t * N : (t + 1) * N]
+            )
+
+        z_grouped, z_codes, z_scale = [], [], []
+        for c, (lo, hi) in enumerate(Z_CHUNKS):
+            z_grouped.append(keep.tile([P, hi - lo, PACK], BF16, name="z_grouped%d" % c, align_bytes=64))
+            z_codes.append(keep.tile([P, hi - lo], U32, name="z_codes%d" % c, align_bytes=64))
+            z_scale.append(keep.tile([P, hi - lo], U8, name="z_scale%d" % c, align_bytes=64))
+
+        def blend(c):
+            lo, hi = Z_CHUNKS[c]
+            h = lo // HALF
+            cols = slice(lo - h * HALF, hi - h * HALF)
+            dst, in0 = side_by_side(z_grouped[c][:], taken[h][:, :, cols])
+            in1 = side_by_side(z_grouped[c][:], kept[h][:, :, cols])[1]
+            nc.vector.tensor_tensor(dst, in0, in1, ALU.subtract)
+
+        def quantise_z(c):
+            nc.vector.quantize_mx(
+                out=z_codes[c][:].bitcast(FP8X4),
+                scales=z_scale[c][:],
+                in_=z_grouped[c][:].rearrange("p c t -> p (c t)"),
+            )
+
+        blend(0)
+        blend(1)
+        quantise_z(0)
+        quantise_w1(0)
+        blend(2)
+        quantise_z(1)
+        quantise_z(2)
+        for t in range(1, PACK):
+            quantise_w1(t)
+
+        out_rows = out.rearrange("(p t) n -> t p n", t=PACK)
+        for t in range(PACK):
+            early = psum.tile([P, H_EARLY], F32, name="h_early", tag="bank0_%d" % t)
+            late = psum.tile([P, H - H_EARLY], F32, name="h_late", tag="bank1_%d" % t)
+            for c, (lo, hi) in enumerate(Z_CHUNKS):
+                nc.tensor.matmul_mx(
+                    out=early[:, lo:hi] if hi <= H_EARLY else late[:],
+                    lhsT=w1_codes[t][:].bitcast(FP8X4),
+                    lhsT_scale=w1_scale[t][:],
+                    rhs=z_codes[c][:].bitcast(FP8X4),
+                    rhs_scale=z_scale[c][:],
+                    start=True,
+                    stop=True,
+                )
+            mixed = keep.tile([P, H], F32, name="mixed%d" % t)
+            nc.scalar.copy(mixed[:, :H_EARLY], early[:])
+            nc.scalar.copy(mixed[:, H_EARLY:], late[:])
+            second, diff = [], []
+            for h in range(2):
+                second.append(ring.tile([P, HALF], F32, name="second%d" % h))
+                nc.vector.tensor_copy(second[h][:], mixed[:].indirect(n4_t[:, list_halves[h]]))
+            for h in range(2):
+                diff.append(ring.tile([P, HALF], F32, name="diff%d" % h))
+                nc.vector.tensor_tensor(
+                    diff[h][:], mixed[:].indirect(n3_t[:, list_halves[h]]), second[h][:], ALU.subtract
+                )
+            for h in range(2):
+                result = keep.tile([P, HALF], F32, name="result%d_%d" % (t, h))
+                nc.vector.tensor_tensor(result[:], diff[h][:], mixed[:, halves[h]], ALU.mult)
+                nc.sync.dma_start(out_rows[t][:, halves[h]], result[:])

@@ -25,10 +25,10 @@ H_EARLY = 384
 SCALE_ROW0 = P - 16
 
 
-def side_by_side(grouped, rows):
+def side_by_side(grouped, rows, run=4):
     return (
-        grouped.rearrange("p (c i) j -> p c j i", i=4),
-        rows.rearrange("p j (c i) -> p c j i", i=4),
+        grouped.rearrange("p (c i) j -> p c j i", i=run),
+        rows.rearrange("p j (c i) -> p c j i", i=run),
     )
 
 
@@ -54,6 +54,9 @@ def tile_picked_toktrackwind_none_p_kernel(
         nc.vector.memset(scale_table[:SCALE_ROW0, :].bitcast(I32), 0)
         x_scale = keep.tile([P, S], U8, align_bytes=64)
         nc.vector.memset(x_scale[:].bitcast(I32), 0)
+        warm = keep.tile([P, 2], F32)
+        nc.gpsimd.memset(warm[:, 0:1], 0.0)
+        nc.scalar.activation(warm[:, 1:2], warm[:, 0:1], ACT.Sigmoid)
         offs_t = load_list(offs, "offs_t")
         word_table = keep.tile([P, T], I32, align_bytes=64)
         nc.sync.dma_start(word_table[:], x_words[0].rearrange("p n r -> p (n r)").bitcast(I32))
@@ -163,8 +166,8 @@ def tile_picked_toktrackwind_none_p_kernel(
             lo, hi = Z_CHUNKS[c]
             h = lo // HALF
             cols = slice(lo - h * HALF, hi - h * HALF)
-            dst, in0 = side_by_side(z_grouped[c][:], taken[h][:, :, cols])
-            in1 = side_by_side(z_grouped[c][:], kept[h][:, :, cols])[1]
+            dst, in0 = side_by_side(z_grouped[c][:], taken[h][:, :, cols], run=2)
+            in1 = side_by_side(z_grouped[c][:], kept[h][:, :, cols], run=2)[1]
             nc.vector.tensor_tensor(dst, in0, in1, ALU.subtract)
 
         def quantise_z(c):
@@ -201,16 +204,19 @@ def tile_picked_toktrackwind_none_p_kernel(
             mixed = keep.tile([P, H], F32, name="mixed%d" % t)
             nc.scalar.copy(mixed[:, :H_EARLY], early[:])
             nc.scalar.copy(mixed[:, H_EARLY:], late[:])
-            second, diff = [], []
+            second = ring.tile([P, H], F32)
+            diff = ring.tile([P, H], F32)
+            result = keep.tile([P, H], F32, name="result%d" % t)
             for h in range(2):
-                second.append(ring.tile([P, HALF], F32, name="second%d" % h))
-                nc.vector.tensor_copy(second[h][:], mixed[:].indirect(n4_t[:, list_halves[h]]))
+                nc.vector.tensor_copy(second[:, halves[h]], mixed[:].indirect(n4_t[:, list_halves[h]]))
             for h in range(2):
-                diff.append(ring.tile([P, HALF], F32, name="diff%d" % h))
                 nc.vector.tensor_tensor(
-                    diff[h][:], mixed[:].indirect(n3_t[:, list_halves[h]]), second[h][:], ALU.subtract
+                    diff[:, halves[h]], mixed[:].indirect(n3_t[:, list_halves[h]]), second[:, halves[h]], ALU.subtract
                 )
-            for h in range(2):
-                result = keep.tile([P, HALF], F32, name="result%d_%d" % (t, h))
-                nc.vector.tensor_tensor(result[:], diff[h][:], mixed[:, halves[h]], ALU.mult)
-                nc.sync.dma_start(out_rows[t][:, halves[h]], result[:])
+            if t < PACK - 1:
+                nc.gpsimd.tensor_tensor(result[:], diff[:], mixed[:], ALU.mult)
+                nc.sync.dma_start(out_rows[t], result[:])
+            else:
+                for h in range(2):
+                    nc.vector.tensor_tensor(result[:, halves[h]], diff[:, halves[h]], mixed[:, halves[h]], ALU.mult)
+                    nc.sync.dma_start(out_rows[t][:, halves[h]], result[:, halves[h]])

@@ -19,7 +19,7 @@ P = 128
 PACK = 4
 HALF = H // 2
 LIST_COLS = HALF // 16
-SCALAR_COLS = 96
+SCALAR_COLS = (128, 96)
 Z_CHUNKS = ((0, 256), (256, 384), (384, 512))
 H_EARLY = 384
 SCALE_ROW0 = P - 16
@@ -95,34 +95,41 @@ def tile_picked_toktrackwind_none_p_kernel(
 
         y = [keep.tile([P, H], F32, name="y%d" % t, tag="y%d" % t, align_bytes=64) for t in range(PACK)]
         gy = [keep.tile([P, H], F32, name="gy%d" % t) for t in range(PACK)]
-        y_banks = {}
+        wa_codes, wa_scale = [], []
         for h in range(2):
+            cut = SCALAR_COLS[h]
             grouped = keep.tile([P, HALF, PACK], BF16, name="wa_grouped%d" % h, align_bytes=64)
-            nc.scalar.copy(*side_by_side(grouped[:, :SCALAR_COLS, :], wa_raw[h][:, :, :SCALAR_COLS]))
-            nc.vector.tensor_copy(*side_by_side(grouped[:, SCALAR_COLS:, :], wa_raw[h][:, :, SCALAR_COLS:]))
-            codes = keep.tile([P, HALF], U32, name="wa_codes%d" % h, align_bytes=64)
-            scale = keep.tile([P, HALF], U8, name="wa_scale%d" % h, align_bytes=64)
+            nc.scalar.copy(*side_by_side(grouped[:, :cut, :], wa_raw[h][:, :, :cut]))
+            nc.vector.tensor_copy(*side_by_side(grouped[:, cut:, :], wa_raw[h][:, :, cut:]))
+            wa_codes.append(keep.tile([P, HALF], U32, name="wa_codes%d" % h, align_bytes=64))
+            wa_scale.append(keep.tile([P, HALF], U8, name="wa_scale%d" % h, align_bytes=64))
             nc.vector.quantize_mx(
-                out=codes[:].bitcast(FP8X4), scales=scale[:], in_=grouped[:].rearrange("p c j -> p (c j)")
+                out=wa_codes[h][:].bitcast(FP8X4),
+                scales=wa_scale[h][:],
+                in_=grouped[:].rearrange("p c j -> p (c j)"),
             )
-            for t in range(PACK):
-                bank = psum.tile([P, HALF], F32, name="y_bank", tag="bank%d_%d" % (h, t))
-                nc.tensor.matmul_mx(
-                    out=bank[:],
-                    lhsT=x_codes[:, t * P : (t + 1) * P].bitcast(FP8X4),
-                    lhsT_scale=x_scale[:, t * P : (t + 1) * P],
-                    rhs=codes[:].bitcast(FP8X4),
-                    rhs_scale=scale[:],
-                    start=True,
-                    stop=True,
-                )
-                y_banks[h, t] = bank
+
+        y_banks = {}
+        for h, t in ((0, 0), (0, 1), (1, 0), (0, 2), (0, 3), (1, 1), (1, 2), (1, 3)):
+            y_banks[h, t] = psum.tile([P, HALF], F32, name="y_bank", tag="bank%d_%d" % (h, t))
+            nc.tensor.matmul_mx(
+                out=y_banks[h, t][:],
+                lhsT=x_codes[:, t * P : (t + 1) * P].bitcast(FP8X4),
+                lhsT_scale=x_scale[:, t * P : (t + 1) * P],
+                rhs=wa_codes[h][:].bitcast(FP8X4),
+                rhs_scale=wa_scale[h][:],
+                start=True,
+                stop=True,
+            )
 
         def gain_on_vector(t, h):
             nc.vector.tensor_scalar(gy[t][:, halves[h]], y[t][:, halves[h]], gain[:, t : t + 1], None, ALU.mult)
 
         for t in range(PACK):
-            nc.scalar.copy(y[t][:, halves[0]], y_banks[0, t][:])
+            if t < 2:
+                nc.scalar.copy(y[t][:, halves[0]], y_banks[0, t][:])
+            else:
+                nc.vector.tensor_copy(y[t][:, halves[0]], y_banks[0, t][:])
             gain_on_vector(t, 0)
 
         taken = [keep.tile([P, PACK, HALF], F32, name="taken%d" % h) for h in range(2)]
@@ -204,19 +211,16 @@ def tile_picked_toktrackwind_none_p_kernel(
             mixed = keep.tile([P, H], F32, name="mixed%d" % t)
             nc.scalar.copy(mixed[:, :H_EARLY], early[:])
             nc.scalar.copy(mixed[:, H_EARLY:], late[:])
-            second = ring.tile([P, H], F32)
-            diff = ring.tile([P, H], F32)
-            result = keep.tile([P, H], F32, name="result%d" % t)
+            second, diff = [], []
             for h in range(2):
-                nc.vector.tensor_copy(second[:, halves[h]], mixed[:].indirect(n4_t[:, list_halves[h]]))
+                second.append(ring.tile([P, HALF], F32, name="second%d" % h))
+                nc.vector.tensor_copy(second[h][:], mixed[:].indirect(n4_t[:, list_halves[h]]))
             for h in range(2):
+                diff.append(ring.tile([P, HALF], F32, name="diff%d" % h))
                 nc.vector.tensor_tensor(
-                    diff[:, halves[h]], mixed[:].indirect(n3_t[:, list_halves[h]]), second[:, halves[h]], ALU.subtract
+                    diff[h][:], mixed[:].indirect(n3_t[:, list_halves[h]]), second[h][:], ALU.subtract
                 )
-            if t < PACK - 1:
-                nc.gpsimd.tensor_tensor(result[:], diff[:], mixed[:], ALU.mult)
-                nc.sync.dma_start(out_rows[t], result[:])
-            else:
-                for h in range(2):
-                    nc.vector.tensor_tensor(result[:, halves[h]], diff[:, halves[h]], mixed[:, halves[h]], ALU.mult)
-                    nc.sync.dma_start(out_rows[t][:, halves[h]], result[:, halves[h]])
+            for h in range(2):
+                result = keep.tile([P, HALF], F32, name="result%d_%d" % (t, h))
+                nc.vector.tensor_tensor(result[:], diff[h][:], mixed[:, halves[h]], ALU.mult)
+                nc.sync.dma_start(out_rows[t][:, halves[h]], result[:])

@@ -41,7 +41,6 @@ def tile_picked_toktrackwind_none_p_kernel(
 
     with ExitStack() as ctx:
         keep = ctx.enter_context(tc.tile_pool(name="keep", bufs=1))
-        ring = ctx.enter_context(tc.tile_pool(name="ring", bufs=2))
         psum = ctx.enter_context(tc.psum_pool(name="psum", bufs=1))
 
         def load_list(source, name):
@@ -150,17 +149,18 @@ def tile_picked_toktrackwind_none_p_kernel(
                     kept[h][:, t, :], gate[:], 1.0, gy[t][:, halves[h]], ALU.subtract, ALU.mult
                 )
 
-        w1_grouped = keep.tile([P, N * PACK], BF16, tag="y2", align_bytes=64)
-        w1_dealt = w1_grouped[:].rearrange("p (t m j) -> p m j t", t=PACK, j=PACK)
         w1_rows = w1_raw[:].rearrange("p j (m t) -> p m j t", t=PACK)
-        for h in range(2):
-            nc.scalar.copy(w1_dealt[:, h * 64 : (h + 1) * 64], w1_rows[:, h * 64 : (h + 1) * 64])
+        w1_first = keep.tile([P, P, PACK], BF16, tag="y2", align_bytes=64)
+        nc.scalar.copy(w1_first[:], w1_rows[:, :, :, 0])
+        w1_rest = keep.tile([P, PACK - 1, P, PACK], BF16, tag="y3", align_bytes=64)
+        nc.scalar.copy(w1_rest[:].rearrange("p t m j -> p m j t"), w1_rows[:, :, :, 1:])
+        w1_grouped = [w1_first[:]] + [w1_rest[:, t] for t in range(PACK - 1)]
         w1_codes = [keep.tile([P, P], U32, name="w1_codes%d" % t, align_bytes=64) for t in range(PACK)]
         w1_scale = [keep.tile([P, P], U8, name="w1_scale%d" % t, align_bytes=64) for t in range(PACK)]
 
         def quantise_w1(t):
             nc.vector.quantize_mx(
-                out=w1_codes[t][:].bitcast(FP8X4), scales=w1_scale[t][:], in_=w1_grouped[:, t * N : (t + 1) * N]
+                out=w1_codes[t][:].bitcast(FP8X4), scales=w1_scale[t][:], in_=w1_grouped[t].rearrange("p m j -> p (m j)")
             )
 
         z_grouped, z_codes, z_scale = [], [], []
@@ -194,7 +194,7 @@ def tile_picked_toktrackwind_none_p_kernel(
         for t in range(1, PACK):
             quantise_w1(t)
 
-        out_rows = out.rearrange("(p t) n -> t p n", t=PACK)
+        mixed, late_banks = [], []
         for t in range(PACK):
             early = psum.tile([P, H_EARLY], F32, name="h_early", tag="bank0_%d" % t)
             late = psum.tile([P, H - H_EARLY], F32, name="h_late", tag="bank1_%d" % t)
@@ -208,19 +208,39 @@ def tile_picked_toktrackwind_none_p_kernel(
                     start=True,
                     stop=True,
                 )
-            mixed = keep.tile([P, H], F32, name="mixed%d" % t)
-            nc.scalar.copy(mixed[:, :H_EARLY], early[:])
-            nc.scalar.copy(mixed[:, H_EARLY:], late[:])
-            second, diff = [], []
+            mixed.append(keep.tile([P, H], F32, name="mixed%d" % t))
+            nc.scalar.copy(mixed[t][:, :H_EARLY], early[:])
+            nc.scalar.copy(mixed[t][:, H_EARLY:], late[:])
+            late_banks.append(late)
+
+        out_rows = out.rearrange("(p t) n -> t p n", t=PACK)
+        second = [keep.tile([P, H], F32, name="second%d" % t) for t in range(PACK)]
+        diff = [keep.tile([P, H], F32, name="diff%d" % t) for t in range(PACK)]
+        result = [keep.tile([P, H], F32, name="result%d" % t) for t in range(PACK)]
+
+        def fetch_second(t):
             for h in range(2):
-                second.append(ring.tile([P, HALF], F32, name="second%d" % h))
-                nc.vector.tensor_copy(second[h][:], mixed[:].indirect(n4_t[:, list_halves[h]]))
+                nc.vector.tensor_copy(second[t][:, halves[h]], mixed[t][:].indirect(n4_t[:, list_halves[h]]))
+
+        def subtract(t):
             for h in range(2):
-                diff.append(ring.tile([P, HALF], F32, name="diff%d" % h))
                 nc.vector.tensor_tensor(
-                    diff[h][:], mixed[:].indirect(n3_t[:, list_halves[h]]), second[h][:], ALU.subtract
+                    diff[t][:, halves[h]],
+                    mixed[t][:].indirect(n3_t[:, list_halves[h]]),
+                    second[t][:, halves[h]],
+                    ALU.subtract,
                 )
-            for h in range(2):
-                result = keep.tile([P, HALF], F32, name="result%d_%d" % (t, h))
-                nc.vector.tensor_tensor(result[:], diff[h][:], mixed[:, halves[h]], ALU.mult)
-                nc.sync.dma_start(out_rows[t][:, halves[h]], result[:])
+
+        fetch_second(0)
+        subtract(0)
+        for t in range(PACK - 1):
+            for cols in (halves[0], slice(HALF, H_EARLY)):
+                nc.gpsimd.tensor_tensor(result[t][:, cols], diff[t][:, cols], mixed[t][:, cols], ALU.mult)
+            fetch_second(t + 1)
+            nc.vector.tensor_tensor(result[t][:, H_EARLY:], diff[t][:, H_EARLY:], late_banks[t][:], ALU.mult)
+            nc.sync.dma_start(out_rows[t], result[t][:])
+            subtract(t + 1)
+        last = PACK - 1
+        for cols in halves:
+            nc.vector.tensor_tensor(result[last][:, cols], diff[last][:, cols], mixed[last][:, cols], ALU.mult)
+            nc.scalar.dma_start(out_rows[last][:, cols], result[last][:, cols])

from contextlib import ExitStack

import concourse.mybir as mybir

K, T, S, N, H = 512, 2048, 512, 512, 512
FLOPS = 2 * K * S * H + 2 * S * N * H

F32 = mybir.dt.float32
BF16 = mybir.dt.bfloat16
I32 = mybir.dt.int32
U32 = mybir.dt.uint32
U16 = mybir.dt.uint16
U8 = mybir.dt.uint8
FP8X4 = mybir.dt.float8_e4m3fn_x4
ALU = mybir.AluOpType
ACT = mybir.ActivationFunctionType

P = 128
PACK = 4
HALF = H // 2
LIST_COLS = HALF // 16
SCALAR_COLS = (128, 96)
Z_CHUNKS = ((0, 256), (256, 384), (384, 512))
H_EARLY = 384
SCALE_ROW0 = P - 16


def side_by_side(grouped, rows, run=4):
    return (
        grouped.rearrange("p (c i) j -> p c j i", i=run),
        rows.rearrange("p j (c i) -> p c j i", i=run),
    )


def tile_picked_toktrackwind_none_p_kernel(
    tc, x_words, x_scales, wa, gt, w1, offs, n1, n2, n3, n4, out
):
    nc = tc.nc
    halves = [slice(h * HALF, (h + 1) * HALF) for h in range(2)]
    list_halves = [slice(h * LIST_COLS, (h + 1) * LIST_COLS) for h in range(2)]

    with ExitStack() as ctx:
        keep = ctx.enter_context(tc.tile_pool(name="keep", bufs=1))
        psum = ctx.enter_context(tc.psum_pool(name="psum", bufs=1))

        def load_list(source, name):
            tile = keep.tile([P, source.shape[1]], U16, name=name)
            nc.sync.dma_start(tile[:], source)
            return tile

        scale_table = keep.tile([P, T], U8, align_bytes=64)
        nc.sync.dma_start(scale_table[SCALE_ROW0:, :].bitcast(I32), x_scales[0].bitcast(I32))
        nc.vector.memset(scale_table[:SCALE_ROW0, :].bitcast(I32), 0)
        x_scale = keep.tile([P, S], U8, align_bytes=64)
        nc.vector.memset(x_scale[:].bitcast(I32), 0)
        warm = keep.tile([P, 2], F32)
        nc.gpsimd.memset(warm[:, 0:1], 0.0)
        nc.scalar.activation(warm[:, 1:2], warm[:, 0:1], ACT.Sigmoid)
        offs_t = load_list(offs, "offs_t")
        word_table = keep.tile([P, T], I32, align_bytes=64)
        nc.sync.dma_start(word_table[:], x_words[0].rearrange("p n r -> p (n r)").bitcast(I32))
        wa_rows = wa.rearrange("(p j) c -> p j c", j=PACK)
        wa_raw = []
        for h in range(2):
            raw = keep.tile([P, PACK, HALF], F32, name="wa_raw%d" % h)
            nc.sync.dma_start(raw[:], wa_rows[:, :, halves[h]])
            wa_raw.append(raw)
        gain = keep.tile([P, PACK], F32)
        nc.sync.dma_start(gain[:], gt.rearrange("(p t) o -> p (t o)", t=PACK))
        n1_t = load_list(n1, "n1_t")
        n2_t = load_list(n2, "n2_t")
        w1_raw = keep.tile([P, PACK, N], F32)
        nc.sync.dma_start(w1_raw[:], w1.rearrange("(p j) m -> p j m", j=PACK))
        n3_t = load_list(n3, "n3_t")
        n4_t = load_list(n4, "n4_t")

        picked_scales = keep.tile([P, S], U8, align_bytes=64)
        nc.vector.tensor_copy(picked_scales[:], scale_table[:].indirect(offs_t[:]))
        dealt_scales = keep.tile([P, S], U8, align_bytes=64)
        nc.vector.tensor_copy(
            dealt_scales[:].rearrange("p (t m) -> p t m", t=PACK),
            picked_scales[:].rearrange("p (m t) -> p t m", t=PACK),
        )
        for q in range(4):
            nc.scalar.dma_start(
                x_scale[32 * q : 32 * q + 4, :].bitcast(I32),
                dealt_scales[SCALE_ROW0 + 4 * q : SCALE_ROW0 + 4 * q + 4, :].bitcast(I32),
            )
        x_codes = keep.tile([P, S], U32, align_bytes=64)
        nc.vector.tensor_copy(
            x_codes[:].rearrange("p (t m) -> p m t", t=PACK),
            word_table[:].bitcast(U32).indirect(offs_t[:]),
        )

        y = [keep.tile([P, H], F32, name="y%d" % t, tag="y%d" % t, align_bytes=64) for t in range(PACK)]
        gy = [keep.tile([P, H], F32, name="gy%d" % t) for t in range(PACK)]
        wa_codes, wa_scale = [], []
        for h in range(2):
            cut = SCALAR_COLS[h]
            grouped = keep.tile([P, HALF, PACK], BF16, name="wa_grouped%d" % h, align_bytes=64)
            nc.scalar.copy(*side_by_side(grouped[:, :cut, :], wa_raw[h][:, :, :cut]))
            nc.vector.tensor_copy(*side_by_side(grouped[:, cut:, :], wa_raw[h][:, :, cut:]))
            wa_codes.append(keep.tile([P, HALF], U32, name="wa_codes%d" % h, align_bytes=64))
            wa_scale.append(keep.tile([P, HALF], U8, name="wa_scale%d" % h, align_bytes=64))
            nc.vector.quantize_mx(
                out=wa_codes[h][:].bitcast(FP8X4),
                scales=wa_scale[h][:],
                in_=grouped[:].rearrange("p c j -> p (c j)"),
            )

        y_banks = {}
        for h, t in ((0, 0), (0, 1), (1, 0), (0, 2), (0, 3), (1, 1), (1, 2), (1, 3)):
            y_banks[h, t] = psum.tile([P, HALF], F32, name="y_bank", tag="bank%d_%d" % (h, t))
            nc.tensor.matmul_mx(
                out=y_banks[h, t][:],
                lhsT=x_codes[:, t * P : (t + 1) * P].bitcast(FP8X4),
                lhsT_scale=x_scale[:, t * P : (t + 1) * P],
                rhs=wa_codes[h][:].bitcast(FP8X4),
                rhs_scale=wa_scale[h][:],
                start=True,
                stop=True,
            )

        def gain_on_vector(t, h):
            nc.vector.tensor_scalar(gy[t][:, halves[h]], y[t][:, halves[h]], gain[:, t : t + 1], None, ALU.mult)

        for t in range(PACK):
            if t < 2:
                nc.scalar.copy(y[t][:, halves[0]], y_banks[0, t][:])
            else:
                nc.vector.tensor_copy(y[t][:, halves[0]], y_banks[0, t][:])
            gain_on_vector(t, 0)

        taken = [keep.tile([P, PACK, HALF], F32, name="taken%d" % h) for h in range(2)]
        kept = [keep.tile([P, PACK, HALF], F32, name="kept%d" % h) for h in range(2)]
        for t in range(PACK):
            nc.scalar.copy(y[t][:, halves[1]], y_banks[1, t][:])
            if t == 0:
                gain_on_vector(t, 1)
            else:
                nc.scalar.activation(gy[t][:, halves[1]], y_banks[1, t][:], ACT.Copy, scale=gain[:, t : t + 1])
            for h in range(2):
                gate = keep.tile([P, HALF], F32, name="gate%d_%d" % (t, h))
                nc.scalar.activation(gate[:], y[t][:].indirect(n1_t[:, list_halves[h]]), ACT.Sigmoid)
                nc.vector.tensor_tensor(
                    taken[h][:, t, :], gy[t][:].indirect(n2_t[:, list_halves[h]]), gate[:], ALU.mult
                )
                nc.vector.scalar_tensor_tensor(
                    kept[h][:, t, :], gate[:], 1.0, gy[t][:, halves[h]], ALU.subtract, ALU.mult
                )

        w1_rows = w1_raw[:].rearrange("p j (m t) -> p m j t", t=PACK)
        w1_first = keep.tile([P, P, PACK], BF16, tag="y2", align_bytes=64)
        nc.scalar.copy(w1_first[:], w1_rows[:, :, :, 0])
        w1_rest = keep.tile([P, PACK - 1, P, PACK], BF16, tag="y3", align_bytes=64)
        nc.scalar.copy(w1_rest[:].rearrange("p t m j -> p m j t"), w1_rows[:, :, :, 1:])
        w1_grouped = [w1_first[:]] + [w1_rest[:, t] for t in range(PACK - 1)]
        w1_codes = [keep.tile([P, P], U32, name="w1_codes%d" % t, align_bytes=64) for t in range(PACK)]
        w1_scale = [keep.tile([P, P], U8, name="w1_scale%d" % t, align_bytes=64) for t in range(PACK)]

        def quantise_w1(t):
            nc.vector.quantize_mx(
                out=w1_codes[t][:].bitcast(FP8X4), scales=w1_scale[t][:], in_=w1_grouped[t].rearrange("p m j -> p (m j)")
            )

        z_grouped, z_codes, z_scale = [], [], []
        for c, (lo, hi) in enumerate(Z_CHUNKS):
            z_grouped.append(keep.tile([P, hi - lo, PACK], BF16, name="z_grouped%d" % c, align_bytes=64))
            z_codes.append(keep.tile([P, hi - lo], U32, name="z_codes%d" % c, align_bytes=64))
            z_scale.append(keep.tile([P, hi - lo], U8, name="z_scale%d" % c, align_bytes=64))

        def blend(c):
            lo, hi = Z_CHUNKS[c]
            h = lo // HALF
            cols = slice(lo - h * HALF, hi - h * HALF)
            dst, in0 = side_by_side(z_grouped[c][:], taken[h][:, :, cols], run=2)
            in1 = side_by_side(z_grouped[c][:], kept[h][:, :, cols], run=2)[1]
            nc.vector.tensor_tensor(dst, in0, in1, ALU.subtract)

        def quantise_z(c):
            nc.vector.quantize_mx(
                out=z_codes[c][:].bitcast(FP8X4),
                scales=z_scale[c][:],
                in_=z_grouped[c][:].rearrange("p c t -> p (c t)"),
            )

        blend(0)
        blend(1)
        quantise_z(0)
        quantise_w1(0)
        blend(2)
        quantise_z(1)
        quantise_z(2)
        for t in range(1, PACK):
            quantise_w1(t)

        mixed, late_banks = [], []
        for t in range(PACK):
            early = psum.tile([P, H_EARLY], F32, name="h_early", tag="bank0_%d" % t)
            late = psum.tile([P, H - H_EARLY], F32, name="h_late", tag="bank1_%d" % t)
            for c, (lo, hi) in enumerate(Z_CHUNKS):
                nc.tensor.matmul_mx(
                    out=early[:, lo:hi] if hi <= H_EARLY else late[:],
                    lhsT=w1_codes[t][:].bitcast(FP8X4),
                    lhsT_scale=w1_scale[t][:],
                    rhs=z_codes[c][:].bitcast(FP8X4),
                    rhs_scale=z_scale[c][:],
                    start=True,
                    stop=True,
                )
            mixed.append(keep.tile([P, H], F32, name="mixed%d" % t))
            nc.scalar.copy(mixed[t][:, :H_EARLY], early[:])
            nc.scalar.copy(mixed[t][:, H_EARLY:], late[:])
            late_banks.append(late)

        out_rows = out.rearrange("(p t) n -> t p n", t=PACK)
        second = [keep.tile([P, H], F32, name="second%d" % t) for t in range(PACK)]
        diff = [keep.tile([P, H], F32, name="diff%d" % t) for t in range(PACK)]
        result = [keep.tile([P, H], F32, name="result%d" % t) for t in range(PACK)]

        def fetch_second(t):
            for h in range(2):
                nc.vector.tensor_copy(second[t][:, halves[h]], mixed[t][:].indirect(n4_t[:, list_halves[h]]))

        def subtract(t):
            for h in range(2):
                nc.vector.tensor_tensor(
                    diff[t][:, halves[h]],
                    mixed[t][:].indirect(n3_t[:, list_halves[h]]),
                    second[t][:, halves[h]],
                    ALU.subtract,
                )

        fetch_second(0)
        subtract(0)
        for t in range(PACK - 1):
            for cols in (halves[0], slice(HALF, H_EARLY)):
                nc.gpsimd.tensor_tensor(result[t][:, cols], diff[t][:, cols], mixed[t][:, cols], ALU.mult)
            fetch_second(t + 1)
            nc.vector.tensor_tensor(result[t][:, H_EARLY:], diff[t][:, H_EARLY:], late_banks[t][:], ALU.mult)
            nc.sync.dma_start(out_rows[t], result[t][:])
            subtract(t + 1)
        last = PACK - 1
        for cols in halves:
            nc.vector.tensor_tensor(result[last][:, cols], diff[last][:, cols], mixed[last][:, cols], ALU.mult)
            nc.scalar.dma_start(out_rows[last][:, cols], result[last][:, cols])
